import numpy as np
import ml_dtypes


def mxq(x, axis, fmt="e4m3"):
    dtype, down = {"e4m3": (ml_dtypes.float8_e4m3fn, 7), "e5m2": (ml_dtypes.float8_e5m2, 14)}[fmt]
    v = np.moveaxis(np.asarray(x, np.float32).astype(ml_dtypes.bfloat16).astype(np.float64), axis, -1)
    blocks = v.reshape(v.shape[:-1] + (-1, 32))
    amax = np.abs(blocks).max(-1, keepdims=True)
    byte = np.maximum(np.where(amax > 0, np.frexp(amax)[1] - 1 + 127, 0) - down, 1)
    scale = np.exp2(byte - 127.0)
    codes = (blocks / scale).astype(np.float32).astype(dtype).astype(np.float64)
    return np.moveaxis((codes * scale).reshape(v.shape), -1, axis)


WIDE = False


def mx_kscale(k):
    if not WIDE:
        return np.ones(k)
    levels = np.array([10, -10, 5, -5, 0])
    if k % 512:
        return np.exp2(np.random.permutation(np.resize(levels, k // 32))).repeat(32)
    a = np.empty((k // 512, 16))
    for p in range(k // 512):
        a[p, :8] = np.random.permutation(np.resize(levels, 8))
        for g in range(8):
            far = levels[np.abs(levels - a[p, g]) >= 10]
            a[p, g + 8] = far[np.random.randint(len(far))]
    return np.exp2(a.ravel()).repeat(32)


def f64(x):
    return np.asarray(x).astype(np.float64)


def striped(idx):
    return np.tile(np.asarray(idx).reshape(-1, 16).T, (8, 1)).astype(np.uint16)


def unstriped(offs):
    return offs[:16].T.reshape(-1).astype(np.int64)


E2M1 = np.array([0.0, 0.5, 1.0, 1.5, 2.0, 3.0, 4.0, 6.0, -0.0, -0.5, -1.0, -1.5, -2.0, -3.0, -4.0, -6.0])


def pack_weight(w, fmt):
    k, n = w.shape
    w = f64(np.asarray(w, np.float32).astype(ml_dtypes.bfloat16)).reshape(k // 32, 32, n)
    amax = np.abs(w).max(1)
    if fmt == "e4m3":
        byte = np.frexp(amax)[1] - 1 + 127 - 7
    else:
        mant, ex = np.frexp(amax / 6.0)
        byte = np.where(mant > 0.5, ex, ex - 1) + 127
    byte = np.clip(np.where(amax > 0, byte, 1), 1, 254)
    scaled = (w * np.exp2(127.0 - byte)[:, None, :]).reshape(k, n).astype(np.float32)
    by_word = np.ascontiguousarray(scaled.reshape(k // 512, 128, 4, n).transpose(0, 1, 3, 2))
    if fmt == "e4m3":
        words = by_word.astype(ml_dtypes.float8_e4m3fn).view(np.uint8)
    else:
        c = by_word.astype(ml_dtypes.float4_e2m1fn).view(np.uint8) & 0xF
        words = (c[..., 0::2] | (c[..., 1::2] << 4)).reshape(k // 512, 128, 2 * n)
    return np.ascontiguousarray(words), np.ascontiguousarray(byte.astype(np.uint8).reshape(k // 512, 16, n))


def unpack_weight(words, scales, fmt):
    g, _, n = scales.shape
    words = np.ascontiguousarray(words).reshape(g, 128, n, -1)
    if fmt == "e4m3":
        vals = words.view(ml_dtypes.float8_e4m3fn).astype(np.float64)
    else:
        nib = np.empty((g, 128, n, 4), np.uint8)
        nib[..., 0::2] = words & 0xF
        nib[..., 1::2] = words >> 4
        vals = E2M1[nib]
    vals = vals * np.repeat(np.exp2(scales.astype(np.float64) - 127.0), 8, axis=1)[..., None]
    return vals.transpose(0, 1, 3, 2).reshape(g * 512, n)


D, E, T, I, Q = 512, 512, 2048, 512, 128


def setup_inputs():
    n = np.random.standard_normal
    idx = np.random.permutation(T)[:I]
    fd = mx_kscale(D)
    fe = mx_kscale(E)
    keysp = pack_weight(n((D, T)) / fd[:, None], "e4m3")
    valsp = pack_weight(n((E, T)) / fe[:, None], "e4m3")
    return {
        "query": (n((D, Q)) * 0.8 / np.sqrt(D) * fd[:, None]).astype(np.float32),
        "keys_words": keysp[0],
        "keys_scales": keysp[1],
        "damp": (np.random.uniform(1.0, 4.0, (Q, 1))).astype(np.float32),
        "gout": (n((E, Q)) * 1 / np.sqrt(E) * fe[:, None]).astype(np.float32),
        "vals_words": valsp[0],
        "vals_scales": valsp[1],
        "dquery": (n((D, Q)) * 1.0 / np.sqrt(D) * fd[:, None]).astype(np.float32),
        "base": (0.5 * n((Q, T))).astype(np.float32),
        "offs": striped(idx),
    }


def reference(query, keys_words, keys_scales, damp, gout, vals_words, vals_scales, dquery, base, offs):
    idx = unstriped(offs)
    keysu = unpack_weight(keys_words, keys_scales, "e4m3")
    valsu = unpack_weight(vals_words, vals_scales, "e4m3")
    queryq = mxq(f64(query), 0, "e4m3")
    keysidxg = keysu[:, idx]
    a = queryq.T @ keysidxg
    dqueryq = mxq(f64(dquery), 0, "e4m3")
    ta = dqueryq.T @ keysidxg
    p = np.exp(a - np.max(a, axis=1, keepdims=True))
    r = p / np.sum(p, axis=1, keepdims=True) * 512.0
    u0 = np.log(r * f64(damp) + 1.0)
    goutq = mxq(f64(gout), 0, "e4m3")
    valsidxg = valsu[:, idx]
    c0 = goutq.T @ valsidxg
    du0 = c0 / np.sum(u0, axis=1, keepdims=True) + np.sum(c0 * u0 / np.square(np.sum(u0, axis=1, keepdims=True)) * (-1.0), axis=1, keepdims=True)
    dr = du0 / (r * f64(damp) + 1.0) * f64(damp)
    dp = dr * 512.0 / np.sum(p, axis=1, keepdims=True) + np.sum(dr * 512.0 * p / np.square(np.sum(p, axis=1, keepdims=True)) * (-1.0), axis=1, keepdims=True)
    tp = ta * p
    tr = (tp - np.sum(tp, axis=1, keepdims=True) * p / np.sum(p, axis=1, keepdims=True)) / np.sum(p, axis=1, keepdims=True) * 512.0
    tu0 = tr * f64(damp) / (r * f64(damp) + 1.0)
    tdu0 = np.sum(tu0, axis=1, keepdims=True) * c0 / np.square(np.sum(u0, axis=1, keepdims=True)) * (-1.0) + np.sum((tu0 * c0 - np.sum(tu0, axis=1, keepdims=True) * np.sum(u0, axis=1, keepdims=True) * 2.0 * c0 * u0 / np.square(np.sum(u0, axis=1, keepdims=True))) / np.square(np.sum(u0, axis=1, keepdims=True)) * (-1.0), axis=1, keepdims=True)
    tdr = (tdu0 - tr * f64(damp) * du0 / (r * f64(damp) + 1.0)) / (r * f64(damp) + 1.0) * f64(damp)
    tdp = (tdr * 512.0 - np.sum(tp, axis=1, keepdims=True) * dr * 512.0 / np.sum(p, axis=1, keepdims=True)) / np.sum(p, axis=1, keepdims=True) + np.sum((tdr * 512.0 * p + tp * dr * 512.0 - np.sum(tp, axis=1, keepdims=True) * np.sum(p, axis=1, keepdims=True) * 2.0 * dr * 512.0 * p / np.square(np.sum(p, axis=1, keepdims=True))) / np.square(np.sum(p, axis=1, keepdims=True)) * (-1.0), axis=1, keepdims=True)
    tda = tdp * p + tp * dp
    gs = tda * 512.0
    gf = np.zeros((Q, T))
    gf[:, idx] = gs
    y = f64(base) + gf
    return y

@@ -1,0 +1,225 @@
+from contextlib import ExitStack
+
+import concourse.mybir as mybir
+
+F32 = mybir.dt.float32
+BF16 = mybir.dt.bfloat16
+I32 = mybir.dt.int32
+U32 = mybir.dt.uint32
+U16 = mybir.dt.uint16
+U8 = mybir.dt.uint8
+FP8X4 = mybir.dt.float8_e4m3fn_x4
+ALU = mybir.AluOpType
+ACT = mybir.ActivationFunctionType
+
+P = 128
+PACK = 4
+TOKENS = 2048
+SLOTS = 512
+ROWS = 128
+HALF = SLOTS // 2
+OUT_CHUNK = 512
+
+FLOPS = 3 * 2 * 512 * ROWS * SLOTS
+
+
+def tile_attend_hvdirect_dampened_s_kernel(
+    tc, query, keys_words, keys_scales, damp, gout, vals_words, vals_scales, dquery, base, offs, out
+):
+    nc = tc.nc
+    with ExitStack() as ctx:
+        sb = ctx.enter_context(tc.tile_pool(name="sb", bufs=1))
+        ps = ctx.enter_context(tc.psum_pool(name="ps", bufs=1))
+
+        def wide(name):
+            return sb.tile([P, SLOTS], F32, name=name)
+
+        def column(name):
+            return sb.tile([P, 1], F32, name=name)
+
+        def load_scale_rows(plane, rows):
+            for quad in range(4):
+                nc.sync.dma_start(
+                    out=plane[32 * quad : 32 * quad + 4, :].bitcast(I32),
+                    in_=rows[0, 4 * quad : 4 * quad + 4, :].bitcast(I32),
+                )
+
+        def load_words(pool_words, words):
+            nc.sync.dma_start(
+                out=pool_words[:].bitcast(I32), in_=words[0].rearrange("p n t -> p (n t)").bitcast(I32)
+            )
+
+        def load_rows(name, matrix):
+            raw = sb.tile([P, PACK, ROWS], F32, name=name)
+            nc.sync.dma_start(out=raw[:], in_=matrix.rearrange("(p j) w -> p j w", j=PACK))
+            return raw
+
+        def quantise(name, raw):
+            grouped = sb.tile([P, ROWS, PACK], BF16, name=name + "_bf16", align_bytes=64)
+            codes = sb.tile([P, ROWS], U32, name=name + "_codes", align_bytes=64)
+            scales = sb.tile([P, ROWS], U8, name=name + "_scales", align_bytes=64)
+            nc.scalar.activation(out=grouped[:], in_=raw[:].rearrange("p j w -> p w j"), func=ACT.Copy)
+            nc.vector.quantize_mx(
+                out=codes[:].bitcast(FP8X4), scales=scales[:], in_=grouped[:].rearrange("p w j -> p (w j)")
+            )
+            return codes, scales
+
+        def product(acc, stationary, words, scales):
+            nc.tensor.matmul_mx(
+                out=acc,
+                lhsT=stationary[0][:].bitcast(FP8X4),
+                lhsT_scale=stationary[1][:],
+                rhs=words.bitcast(FP8X4),
+                rhs_scale=scales,
+                start=True,
+                stop=True,
+            )
+
+        offsets = sb.tile([P, SLOTS // 16], U16, name="offsets")
+        key_pool = sb.tile([P, TOKENS], U32, name="key_pool", align_bytes=64)
+        key_pool_scales = sb.tile([P, TOKENS], U8, name="key_pool_scales", align_bytes=64)
+        val_pool = sb.tile([P, TOKENS], U32, name="val_pool", align_bytes=64)
+        val_pool_scales = sb.tile([P, TOKENS], U8, name="val_pool_scales", align_bytes=64)
+        placed = sb.tile([P, TOKENS], F32, name="placed")
+        base_sb = sb.tile([P, TOKENS], F32, name="base_sb")
+        damp_sb = column("damp_sb")
+
+        nc.vector.memset(key_pool_scales[:].bitcast(I32), 0)
+        nc.vector.memset(val_pool_scales[:].bitcast(I32), 0)
+        nc.vector.memset(placed[:], 0.0)
+
+        nc.sync.dma_start(offsets[:], offs)
+        query_raw = load_rows("query_raw", query)
+        load_scale_rows(key_pool_scales, keys_scales)
+        load_words(key_pool, keys_words)
+        dquery_raw = load_rows("dquery_raw", dquery)
+        gout_raw = load_rows("gout_raw", gout)
+        nc.sync.dma_start(out=damp_sb[:], in_=damp)
+        load_scale_rows(val_pool_scales, vals_scales)
+        load_words(val_pool, vals_words)
+        nc.sync.dma_start(out=base_sb[:], in_=base)
+
+        key_words = sb.tile([P, SLOTS], U32, name="key_words", align_bytes=64)
+        key_scales = sb.tile([P, SLOTS], U8, name="key_scales", align_bytes=64)
+        nc.vector.tensor_copy(key_scales[:], key_pool_scales[:].indirect(offsets[:]))
+        query_mx = quantise("query", query_raw)
+        halves = [slice(0, HALF), slice(HALF, SLOTS)]
+        score = [ps.tile([P, HALF], F32, name="score%d" % h) for h in range(2)]
+        for h, cols in enumerate(halves):
+            nc.vector.tensor_copy(
+                key_words[:, cols], key_pool[:].indirect(offsets[:, cols.start // 16 : cols.stop // 16])
+            )
+            product(score[h][:], query_mx, key_words[:, cols], key_scales[:, cols])
+        neg_a = wide("neg_a")
+        neg_max_first = column("neg_max_first")
+        neg_max = column("neg_max")
+        nc.vector.tensor_scalar(
+            out=neg_a[:, halves[0]], in0=score[0][:], scalar1=-1.0, scalar2=None,
+            op0=ALU.mult, op1=ALU.min, accum_out=neg_max_first[:],
+        )
+        nc.vector.tensor_scalar(
+            out=neg_a[:, halves[1]], in0=score[1][:], scalar1=-1.0, scalar2=neg_max_first[:],
+            op0=ALU.mult, op1=ALU.min, accum_out=neg_max[:],
+        )
+        dquery_mx = quantise("dquery", dquery_raw)
+        gout_mx = quantise("gout", gout_raw)
+        ta = ps.tile([P, SLOTS], F32, name="ta")
+        product(ta[:], dquery_mx, key_words[:], key_scales[:])
+
+        p = wide("p")
+        p_sum = column("p_sum")
+        nc.scalar.activation(out=p[:], in_=neg_a[:], func=ACT.Exp, scale=-1.0, bias=neg_max[:], accum_out=p_sum[:])
+        inv_p = column("inv_p")
+        k = column("k")
+        neg_inv_p = column("neg_inv_p")
+        nc.vector.reciprocal(out=inv_p[:], in_=p_sum[:])
+        nc.vector.tensor_scalar(out=k[:], in0=inv_p[:], scalar1=damp_sb[:], scalar2=512.0, op0=ALU.mult, op1=ALU.mult)
+        u0 = wide("u0")
+        u_sum = column("u_sum")
+        nc.scalar.activation(out=u0[:], in_=p[:], func=ACT.Ln, scale=k[:], bias=1.0, accum_out=u_sum[:])
+
+        nc.vector.tensor_scalar(out=neg_inv_p[:], in0=inv_p[:], scalar1=-1.0, scalar2=None, op0=ALU.mult)
+        neg_s_ta = wide("neg_s_ta")
+        neg_t = column("neg_t")
+        nc.vector.scalar_tensor_tensor(
+            out=neg_s_ta[:], in0=ta[:], scalar=neg_inv_p[:], in1=p[:], op0=ALU.mult, op1=ALU.mult, accum_out=neg_t[:]
+        )
+
+        val_words = sb.tile([P, SLOTS], U32, name="val_words", align_bytes=64)
+        val_scales = sb.tile([P, SLOTS], U8, name="val_scales", align_bytes=64)
+        nc.vector.tensor_copy(val_scales[:], val_pool_scales[:].indirect(offsets[:]))
+        nc.vector.tensor_copy(val_words[:], val_pool[:].indirect(offsets[:]))
+        c0 = ps.tile([P, SLOTS], F32, name="c0")
+        product(c0[:], gout_mx, val_words[:], val_scales[:])
+
+        u0_less_a = wide("u0_less_a")
+        nc.vector.tensor_tensor(out=u0_less_a[:], in0=neg_a[:], in1=u0[:], op=ALU.add)
+        pw = wide("pw")
+        pw_sum = column("pw_sum")
+        w = wide("w")
+        nc.scalar.activation(
+            out=pw[:], in_=u0_less_a[:], func=ACT.Exp, scale=-1.0, bias=neg_max[:], accum_out=pw_sum[:]
+        )
+        nc.scalar.activation(out=w[:], in_=u0[:], func=ACT.Exp, scale=-1.0)
+
+        inv_u = column("inv_u")
+        c = column("c")
+        neg_ck = column("neg_ck")
+        c_neg_t = column("c_neg_t")
+        m = column("m")
+        c0_u0 = wide("c0_u0")
+        nc.vector.reciprocal(out=inv_u[:], in_=u_sum[:])
+        nc.vector.scalar_tensor_tensor(
+            out=c0_u0[:], in0=c0[:], scalar=inv_u[:], in1=u0[:], op0=ALU.mult, op1=ALU.mult, accum_out=m[:]
+        )
+        nc.vector.tensor_scalar(out=c[:], in0=inv_u[:], scalar1=k[:], scalar2=512.0, op0=ALU.mult, op1=ALU.mult)
+        nc.vector.tensor_scalar(out=neg_ck[:], in0=c[:], scalar1=c[:], scalar2=-1.0 / 512.0, op0=ALU.mult, op1=ALU.mult)
+        nc.vector.tensor_scalar(out=c_neg_t[:], in0=c[:], scalar1=neg_t[:], scalar2=None, op0=ALU.mult)
+
+        y2, y1, y3, y4 = wide("y2"), wide("y1"), wide("y3"), wide("y4")
+        tu_sum, h_sum, tm_sum, v_sum = column("tu_sum"), column("h_sum"), column("tm_sum"), column("v_sum")
+        nc.vector.scalar_tensor_tensor(
+            out=y2[:], in0=ta[:], scalar=neg_t[:], in1=pw[:], op0=ALU.add, op1=ALU.mult, accum_out=tu_sum[:]
+        )
+        nc.vector.scalar_tensor_tensor(
+            out=y1[:], in0=c0[:], scalar=m[:], in1=pw[:], op0=ALU.subtract, op1=ALU.mult, accum_out=h_sum[:]
+        )
+        nc.vector.scalar_tensor_tensor(
+            out=y3[:], in0=ta[:], scalar=neg_t[:], in1=y1[:], op0=ALU.add, op1=ALU.mult, accum_out=tm_sum[:]
+        )
+        nc.vector.scalar_tensor_tensor(
+            out=y4[:], in0=y3[:], scalar=c[:], in1=w[:], op0=ALU.mult, op1=ALU.mult, accum_out=v_sum[:]
+        )
+
+        def affine(name, x, scale, bias=None):
+            y = column(name)
+            if bias is None:
+                nc.scalar.activation(out=y[:], in_=x[:], func=ACT.Copy, scale=scale[:])
+            else:
+                nc.scalar.activation(out=y[:], in_=x[:], func=ACT.Identity, scale=scale[:], bias=bias[:])
+            return y
+
+        coef_y1 = affine("coef_y1", tu_sum, neg_ck)
+        coef_h = affine("coef_h", tu_sum, neg_ck, c_neg_t)
+        coef_ta = affine("coef_ta", h_sum, c)
+        part1 = affine("part1", h_sum, coef_h)
+        coef_pw = affine("coef_pw", tm_sum, neg_ck)
+        part2 = affine("part2", pw_sum, coef_pw, part1)
+        part3 = affine("part3", part2, neg_inv_p)
+        coef_p = affine("coef_p", v_sum, neg_inv_p, part3)
+        p_term = wide("p_term")
+        nc.scalar.activation(out=p_term[:], in_=p[:], func=ACT.Copy, scale=coef_p[:])
+
+        f1, f2, f3 = wide("f1"), wide("f2"), wide("f3")
+        nc.vector.scalar_tensor_tensor(out=f1[:], in0=y1[:], scalar=coef_y1[:], in1=y4[:], op0=ALU.mult, op1=ALU.add)
+        nc.vector.scalar_tensor_tensor(out=f2[:], in0=pw[:], scalar=coef_pw[:], in1=f1[:], op0=ALU.mult, op1=ALU.add)
+        nc.vector.scalar_tensor_tensor(
+            out=f3[:], in0=neg_s_ta[:], scalar=coef_ta[:], in1=f2[:], op0=ALU.mult, op1=ALU.add
+        )
+        nc.vector.tensor_tensor(out=placed[:].indirect(offsets[:]), in0=f3[:], in1=p_term[:], op=ALU.add)
+
+        for j in range(TOKENS // OUT_CHUNK):
+            cols = slice(j * OUT_CHUNK, (j + 1) * OUT_CHUNK)
+            result = sb.tile([P, OUT_CHUNK], F32, name="result%d" % j)
+            nc.vector.tensor_tensor(out=result[:], in0=base_sb[:, cols], in1=placed[:, cols], op=ALU.add)
+            nc.sync.dma_start(out=out[:, cols], in_=result[:])

@@ -18,7 +18,7 @@ TOKENS = 2048
 SLOTS = 512
 ROWS = 128
 HALF = SLOTS // 2
-OUT_CHUNK = 512
+OUT_EDGES = (0, 256, 768, 1280, 1792, 2048)
 
 FLOPS = 3 * 2 * 512 * ROWS * SLOTS
 
@@ -50,25 +50,28 @@ def tile_attend_hvdirect_dampened_s_kernel(
             )
 
         def load_rows(name, matrix):
-            raw = sb.tile([P, PACK, ROWS], F32, name=name)
+            raw = sb.tile([P, PACK, ROWS], F32, name=name, tag=name)
             nc.sync.dma_start(out=raw[:], in_=matrix.rearrange("(p j) w -> p j w", j=PACK))
             return raw
 
-        def quantise(name, raw):
-            grouped = sb.tile([P, ROWS, PACK], BF16, name=name + "_bf16", align_bytes=64)
-            codes = sb.tile([P, ROWS], U32, name=name + "_codes", align_bytes=64)
-            scales = sb.tile([P, ROWS], U8, name=name + "_scales", align_bytes=64)
-            nc.scalar.activation(out=grouped[:], in_=raw[:].rearrange("p j w -> p w j"), func=ACT.Copy)
+        def quantise(name, raws):
+            width = ROWS * len(raws)
+            grouped = sb.tile([P, width, PACK], BF16, name=name + "_bf16", align_bytes=64)
+            codes = sb.tile([P, width], U32, name=name + "_codes", align_bytes=64)
+            scales = sb.tile([P, width], U8, name=name + "_scales", align_bytes=64)
+            spans = [slice(ROWS * i, ROWS * (i + 1)) for i in range(len(raws))]
+            for raw, span in zip(raws, spans):
+                nc.scalar.activation(out=grouped[:, span, :], in_=raw[:].rearrange("p j w -> p w j"), func=ACT.Copy)
             nc.vector.quantize_mx(
                 out=codes[:].bitcast(FP8X4), scales=scales[:], in_=grouped[:].rearrange("p w j -> p (w j)")
             )
-            return codes, scales
+            return [(codes[:, span], scales[:, span]) for span in spans]
 
         def product(acc, stationary, words, scales):
             nc.tensor.matmul_mx(
                 out=acc,
-                lhsT=stationary[0][:].bitcast(FP8X4),
-                lhsT_scale=stationary[1][:],
+                lhsT=stationary[0].bitcast(FP8X4),
+                lhsT_scale=stationary[1],
                 rhs=words.bitcast(FP8X4),
                 rhs_scale=scales,
                 start=True,
@@ -76,33 +79,31 @@ def tile_attend_hvdirect_dampened_s_kernel(
             )
 
         offsets = sb.tile([P, SLOTS // 16], U16, name="offsets")
-        key_pool = sb.tile([P, TOKENS], U32, name="key_pool", align_bytes=64)
+        key_pool = sb.tile([P, TOKENS], U32, name="key_pool", tag="key_pool_bytes", align_bytes=64)
         key_pool_scales = sb.tile([P, TOKENS], U8, name="key_pool_scales", align_bytes=64)
-        val_pool = sb.tile([P, TOKENS], U32, name="val_pool", align_bytes=64)
-        val_pool_scales = sb.tile([P, TOKENS], U8, name="val_pool_scales", align_bytes=64)
+        val_pool = sb.tile([P, TOKENS], U32, name="val_pool", tag="val_pool_bytes", align_bytes=64)
+        val_pool_scales = sb.tile([P, TOKENS], U8, name="val_pool_scales", tag="val_scale_bytes", align_bytes=64)
         placed = sb.tile([P, TOKENS], F32, name="placed")
-        base_sb = sb.tile([P, TOKENS], F32, name="base_sb")
         damp_sb = column("damp_sb")
 
         nc.vector.memset(key_pool_scales[:].bitcast(I32), 0)
         nc.vector.memset(val_pool_scales[:].bitcast(I32), 0)
         nc.vector.memset(placed[:], 0.0)
 
+        nc.gpsimd.dma_start(out=damp_sb[:], in_=damp)
         nc.sync.dma_start(offsets[:], offs)
         query_raw = load_rows("query_raw", query)
         load_scale_rows(key_pool_scales, keys_scales)
         load_words(key_pool, keys_words)
         dquery_raw = load_rows("dquery_raw", dquery)
         gout_raw = load_rows("gout_raw", gout)
-        nc.sync.dma_start(out=damp_sb[:], in_=damp)
         load_scale_rows(val_pool_scales, vals_scales)
         load_words(val_pool, vals_words)
-        nc.sync.dma_start(out=base_sb[:], in_=base)
 
         key_words = sb.tile([P, SLOTS], U32, name="key_words", align_bytes=64)
         key_scales = sb.tile([P, SLOTS], U8, name="key_scales", align_bytes=64)
         nc.vector.tensor_copy(key_scales[:], key_pool_scales[:].indirect(offsets[:]))
-        query_mx = quantise("query", query_raw)
+        (query_mx,) = quantise("query", [query_raw])
         halves = [slice(0, HALF), slice(HALF, SLOTS)]
         score = [ps.tile([P, HALF], F32, name="score%d" % h) for h in range(2)]
         for h, cols in enumerate(halves):
@@ -110,8 +111,10 @@ def tile_attend_hvdirect_dampened_s_kernel(
                 key_words[:, cols], key_pool[:].indirect(offsets[:, cols.start // 16 : cols.stop // 16])
             )
             product(score[h][:], query_mx, key_words[:, cols], key_scales[:, cols])
+        base_sb = sb.tile([P, TOKENS], F32, name="base_sb", tag="key_pool_bytes", align_bytes=64)
+        nc.sync.dma_start(out=base_sb[:], in_=base)
         neg_a = wide("neg_a")
-        neg_max_first = column("neg_max_first")
+        neg_max_first = sb.tile([P, 1], F32, name="neg_max_first", tag="first_max_bytes", align_bytes=64)
         neg_max = column("neg_max")
         nc.vector.tensor_scalar(
             out=neg_a[:, halves[0]], in0=score[0][:], scalar1=-1.0, scalar2=None,
@@ -121,75 +124,61 @@ def tile_attend_hvdirect_dampened_s_kernel(
             out=neg_a[:, halves[1]], in0=score[1][:], scalar1=-1.0, scalar2=neg_max_first[:],
             op0=ALU.mult, op1=ALU.min, accum_out=neg_max[:],
         )
-        dquery_mx = quantise("dquery", dquery_raw)
-        gout_mx = quantise("gout", gout_raw)
+        val_scales = sb.tile([P, SLOTS], U8, name="val_scales", tag="first_max_bytes", align_bytes=64)
+        nc.vector.tensor_copy(val_scales[:], val_pool_scales[:].indirect(offsets[:]))
+        dquery_mx, gout_mx = quantise("dquery_gout", [dquery_raw, gout_raw])
         ta = ps.tile([P, SLOTS], F32, name="ta")
         product(ta[:], dquery_mx, key_words[:], key_scales[:])
 
-        p = wide("p")
+        p = sb.tile([P, SLOTS], F32, name="p", tag="gout_raw")
         p_sum = column("p_sum")
         nc.scalar.activation(out=p[:], in_=neg_a[:], func=ACT.Exp, scale=-1.0, bias=neg_max[:], accum_out=p_sum[:])
-        inv_p = column("inv_p")
+        inv_p = sb.tile([P, 1], F32, name="inv_p", tag="val_scale_bytes", align_bytes=64)
+        nc.vector.reciprocal(out=inv_p[:], in_=p_sum[:])
         k = column("k")
         neg_inv_p = column("neg_inv_p")
-        nc.vector.reciprocal(out=inv_p[:], in_=p_sum[:])
         nc.vector.tensor_scalar(out=k[:], in0=inv_p[:], scalar1=damp_sb[:], scalar2=512.0, op0=ALU.mult, op1=ALU.mult)
         u0 = wide("u0")
         u_sum = column("u_sum")
         nc.scalar.activation(out=u0[:], in_=p[:], func=ACT.Ln, scale=k[:], bias=1.0, accum_out=u_sum[:])
 
         nc.vector.tensor_scalar(out=neg_inv_p[:], in0=inv_p[:], scalar1=-1.0, scalar2=None, op0=ALU.mult)
-        neg_s_ta = wide("neg_s_ta")
-        neg_t = column("neg_t")
-        nc.vector.scalar_tensor_tensor(
-            out=neg_s_ta[:], in0=ta[:], scalar=neg_inv_p[:], in1=p[:], op0=ALU.mult, op1=ALU.mult, accum_out=neg_t[:]
-        )
-
         val_words = sb.tile([P, SLOTS], U32, name="val_words", align_bytes=64)
-        val_scales = sb.tile([P, SLOTS], U8, name="val_scales", align_bytes=64)
-        nc.vector.tensor_copy(val_scales[:], val_pool_scales[:].indirect(offsets[:]))
         nc.vector.tensor_copy(val_words[:], val_pool[:].indirect(offsets[:]))
         c0 = ps.tile([P, SLOTS], F32, name="c0")
         product(c0[:], gout_mx, val_words[:], val_scales[:])
 
-        u0_less_a = wide("u0_less_a")
-        nc.vector.tensor_tensor(out=u0_less_a[:], in0=neg_a[:], in1=u0[:], op=ALU.add)
+        after_gather = sb.tile([P, 2 * SLOTS + 8], F32, name="after_gather", tag="val_pool_bytes", align_bytes=64)
+        neg_s_ta = after_gather[:, 0:SLOTS]
+        u0_less_a = after_gather[:, SLOTS : 2 * SLOTS]
+        inv_u = after_gather[:, 2 * SLOTS : 2 * SLOTS + 1]
+        neg_t = column("neg_t")
+        nc.vector.scalar_tensor_tensor(
+            out=neg_s_ta, in0=ta[:], scalar=neg_inv_p[:], in1=p[:], op0=ALU.mult, op1=ALU.mult, accum_out=neg_t[:]
+        )
+        nc.vector.reciprocal(out=inv_u, in_=u_sum[:])
+        nc.vector.tensor_tensor(out=u0_less_a, in0=neg_a[:], in1=u0[:], op=ALU.add)
         pw = wide("pw")
         pw_sum = column("pw_sum")
         w = wide("w")
         nc.scalar.activation(
-            out=pw[:], in_=u0_less_a[:], func=ACT.Exp, scale=-1.0, bias=neg_max[:], accum_out=pw_sum[:]
+            out=pw[:], in_=u0_less_a, func=ACT.Exp, scale=-1.0, bias=neg_max[:], accum_out=pw_sum[:]
         )
         nc.scalar.activation(out=w[:], in_=u0[:], func=ACT.Exp, scale=-1.0)
 
-        inv_u = column("inv_u")
         c = column("c")
-        neg_ck = column("neg_ck")
-        c_neg_t = column("c_neg_t")
+        neg_kappa = column("neg_kappa")
         m = column("m")
         c0_u0 = wide("c0_u0")
-        nc.vector.reciprocal(out=inv_u[:], in_=u_sum[:])
         nc.vector.scalar_tensor_tensor(
-            out=c0_u0[:], in0=c0[:], scalar=inv_u[:], in1=u0[:], op0=ALU.mult, op1=ALU.mult, accum_out=m[:]
+            out=c0_u0[:], in0=c0[:], scalar=inv_u, in1=u0[:], op0=ALU.mult, op1=ALU.mult, accum_out=m[:]
         )
-        nc.vector.tensor_scalar(out=c[:], in0=inv_u[:], scalar1=k[:], scalar2=512.0, op0=ALU.mult, op1=ALU.mult)
-        nc.vector.tensor_scalar(out=neg_ck[:], in0=c[:], scalar1=c[:], scalar2=-1.0 / 512.0, op0=ALU.mult, op1=ALU.mult)
-        nc.vector.tensor_scalar(out=c_neg_t[:], in0=c[:], scalar1=neg_t[:], scalar2=None, op0=ALU.mult)
-
-        y2, y1, y3, y4 = wide("y2"), wide("y1"), wide("y3"), wide("y4")
-        tu_sum, h_sum, tm_sum, v_sum = column("tu_sum"), column("h_sum"), column("tm_sum"), column("v_sum")
-        nc.vector.scalar_tensor_tensor(
-            out=y2[:], in0=ta[:], scalar=neg_t[:], in1=pw[:], op0=ALU.add, op1=ALU.mult, accum_out=tu_sum[:]
-        )
-        nc.vector.scalar_tensor_tensor(
-            out=y1[:], in0=c0[:], scalar=m[:], in1=pw[:], op0=ALU.subtract, op1=ALU.mult, accum_out=h_sum[:]
-        )
-        nc.vector.scalar_tensor_tensor(
-            out=y3[:], in0=ta[:], scalar=neg_t[:], in1=y1[:], op0=ALU.add, op1=ALU.mult, accum_out=tm_sum[:]
-        )
-        nc.vector.scalar_tensor_tensor(
-            out=y4[:], in0=y3[:], scalar=c[:], in1=w[:], op0=ALU.mult, op1=ALU.mult, accum_out=v_sum[:]
-        )
+        nc.vector.tensor_scalar(out=c[:], in0=inv_u, scalar1=k[:], scalar2=512.0, op0=ALU.mult, op1=ALU.mult)
+        nc.vector.tensor_scalar(out=neg_kappa[:], in0=inv_u, scalar1=k[:], scalar2=-1.0, op0=ALU.mult, op1=ALU.mult)
+        kappa_over_p = column("kappa_over_p")
+        t_over_p = column("t_over_p")
+        nc.vector.tensor_scalar(out=t_over_p[:], in0=neg_t[:], scalar1=neg_inv_p[:], scalar2=None, op0=ALU.mult)
+        nc.vector.tensor_scalar(out=kappa_over_p[:], in0=neg_kappa[:], scalar1=neg_inv_p[:], scalar2=None, op0=ALU.mult)
 
         def affine(name, x, scale, bias=None):
             y = column(name)
@@ -199,27 +188,36 @@ def tile_attend_hvdirect_dampened_s_kernel(
                 nc.scalar.activation(out=y[:], in_=x[:], func=ACT.Identity, scale=scale[:], bias=bias[:])
             return y
 
-        coef_y1 = affine("coef_y1", tu_sum, neg_ck)
-        coef_h = affine("coef_h", tu_sum, neg_ck, c_neg_t)
-        coef_ta = affine("coef_ta", h_sum, c)
-        part1 = affine("part1", h_sum, coef_h)
-        coef_pw = affine("coef_pw", tm_sum, neg_ck)
-        part2 = affine("part2", pw_sum, coef_pw, part1)
-        part3 = affine("part3", part2, neg_inv_p)
-        coef_p = affine("coef_p", v_sum, neg_inv_p, part3)
-        p_term = wide("p_term")
-        nc.scalar.activation(out=p_term[:], in_=p[:], func=ACT.Copy, scale=coef_p[:])
-
-        f1, f2, f3 = wide("f1"), wide("f2"), wide("f3")
-        nc.vector.scalar_tensor_tensor(out=f1[:], in0=y1[:], scalar=coef_y1[:], in1=y4[:], op0=ALU.mult, op1=ALU.add)
-        nc.vector.scalar_tensor_tensor(out=f2[:], in0=pw[:], scalar=coef_pw[:], in1=f1[:], op0=ALU.mult, op1=ALU.add)
+        y2, y1, y1c, y3, z, j_term = wide("y2"), wide("y1"), wide("y1c"), wide("y3"), wide("z"), wide("j_term")
+        tu_sum, coef_ta, tm_sum, j_sum = column("tu_sum"), column("coef_ta"), column("tm_sum"), column("j_sum")
+        nc.vector.scalar_tensor_tensor(out=y1[:], in0=c0[:], scalar=m[:], in1=pw[:], op0=ALU.subtract, op1=ALU.mult)
+        nc.scalar.activation(out=y1c[:], in_=y1[:], func=ACT.Copy, scale=c[:], accum_out=coef_ta[:])
         nc.vector.scalar_tensor_tensor(
-            out=f3[:], in0=neg_s_ta[:], scalar=coef_ta[:], in1=f2[:], op0=ALU.mult, op1=ALU.add
+            out=y2[:], in0=ta[:], scalar=neg_t[:], in1=pw[:], op0=ALU.add, op1=ALU.mult, accum_out=tu_sum[:]
         )
-        nc.vector.tensor_tensor(out=placed[:].indirect(offsets[:]), in0=f3[:], in1=p_term[:], op=ALU.add)
+        nc.vector.scalar_tensor_tensor(out=z[:], in0=ta[:], scalar=neg_t[:], in1=w[:], op0=ALU.add, op1=ALU.mult)
+        nc.vector.scalar_tensor_tensor(
+            out=y3[:], in0=ta[:], scalar=neg_t[:], in1=y1c[:], op0=ALU.add, op1=ALU.mult, accum_out=tm_sum[:]
+        )
+        coef_y1 = affine("coef_y1", tu_sum, neg_kappa)
+        per_tm = affine("per_tm", pw_sum, kappa_over_p)
+        part1 = affine("part1", coef_ta, t_over_p)
+        ta_term = wide("ta_term")
+        nc.scalar.activation(out=ta_term[:], in_=neg_s_ta, func=ACT.Copy, scale=coef_ta[:])
+        nc.vector.scalar_tensor_tensor(
+            out=j_term[:], in0=z[:], scalar=coef_y1[:], in1=y1c[:], op0=ALU.add, op1=ALU.mult, accum_out=j_sum[:]
+        )
+        coef_pw = affine("coef_pw", tm_sum, neg_kappa)
+        part2 = affine("part2", tm_sum, per_tm, part1)
+        coef_p = affine("coef_p", j_sum, neg_inv_p, part2)
 
-        for j in range(TOKENS // OUT_CHUNK):
-            cols = slice(j * OUT_CHUNK, (j + 1) * OUT_CHUNK)
-            result = sb.tile([P, OUT_CHUNK], F32, name="result%d" % j)
+        f1, f2 = wide("f1"), wide("f2")
+        nc.vector.scalar_tensor_tensor(out=f1[:], in0=pw[:], scalar=coef_pw[:], in1=ta_term[:], op0=ALU.mult, op1=ALU.add)
+        nc.vector.scalar_tensor_tensor(out=f2[:], in0=p[:], scalar=coef_p[:], in1=j_term[:], op0=ALU.mult, op1=ALU.add)
+        nc.vector.tensor_tensor(out=placed[:].indirect(offsets[:]), in0=f1[:], in1=f2[:], op=ALU.add)
+
+        for j in range(len(OUT_EDGES) - 1):
+            cols = slice(OUT_EDGES[j], OUT_EDGES[j + 1])
+            result = sb.tile([P, cols.stop - cols.start], F32, name="result%d" % j)
             nc.vector.tensor_tensor(out=result[:], in0=base_sb[:, cols], in1=placed[:, cols], op=ALU.add)
             nc.sync.dma_start(out=out[:, cols], in_=result[:])

@@ -29,6 +29,7 @@ def tile_attend_hvdirect_dampened_s_kernel(
     nc = tc.nc
     with ExitStack() as ctx:
         sb = ctx.enter_context(tc.tile_pool(name="sb", bufs=1))
+        reused = ctx.enter_context(tc.tile_pool(name="reused", bufs=1))
         ps = ctx.enter_context(tc.psum_pool(name="ps", bufs=1))
 
         def wide(name):
@@ -54,18 +55,21 @@ def tile_attend_hvdirect_dampened_s_kernel(
             nc.sync.dma_start(out=raw[:], in_=matrix.rearrange("(p j) w -> p j w", j=PACK))
             return raw
 
-        def quantise(name, raws):
-            width = ROWS * len(raws)
-            grouped = sb.tile([P, width, PACK], BF16, name=name + "_bf16", align_bytes=64)
-            codes = sb.tile([P, width], U32, name=name + "_codes", align_bytes=64)
-            scales = sb.tile([P, width], U8, name=name + "_scales", align_bytes=64)
-            spans = [slice(ROWS * i, ROWS * (i + 1)) for i in range(len(raws))]
-            for raw, span in zip(raws, spans):
-                nc.scalar.activation(out=grouped[:, span, :], in_=raw[:].rearrange("p j w -> p w j"), func=ACT.Copy)
+        def round_and_group(name, raws):
+            grouped = sb.tile([P, ROWS * len(raws), PACK], BF16, name=name, align_bytes=64)
+            for i, raw in enumerate(raws):
+                nc.scalar.activation(
+                    out=grouped[:, ROWS * i : ROWS * (i + 1), :], in_=raw[:].rearrange("p j w -> p w j"), func=ACT.Copy
+                )
+            return grouped
+
+        def quantise(name, grouped, scales):
+            width = grouped.shape[1]
+            codes = sb.tile([P, width], U32, name=name, align_bytes=64)
             nc.vector.quantize_mx(
                 out=codes[:].bitcast(FP8X4), scales=scales[:], in_=grouped[:].rearrange("p w j -> p (w j)")
             )
-            return [(codes[:, span], scales[:, span]) for span in spans]
+            return [(codes[:, s : s + ROWS], scales[:, s : s + ROWS]) for s in range(0, width, ROWS)]
 
         def product(acc, stationary, words, scales):
             nc.tensor.matmul_mx(
@@ -82,7 +86,7 @@ def tile_attend_hvdirect_dampened_s_kernel(
         key_pool = sb.tile([P, TOKENS], U32, name="key_pool", tag="key_pool_bytes", align_bytes=64)
         key_pool_scales = sb.tile([P, TOKENS], U8, name="key_pool_scales", align_bytes=64)
         val_pool = sb.tile([P, TOKENS], U32, name="val_pool", tag="val_pool_bytes", align_bytes=64)
-        val_pool_scales = sb.tile([P, TOKENS], U8, name="val_pool_scales", tag="val_scale_bytes", align_bytes=64)
+        val_pool_scales = reused.tile([P, TOKENS], U8, name="val_pool_scales", align_bytes=64, offset=0)
         placed = sb.tile([P, TOKENS], F32, name="placed")
         damp_sb = column("damp_sb")
 
@@ -103,7 +107,8 @@ def tile_attend_hvdirect_dampened_s_kernel(
         key_words = sb.tile([P, SLOTS], U32, name="key_words", align_bytes=64)
         key_scales = sb.tile([P, SLOTS], U8, name="key_scales", align_bytes=64)
         nc.vector.tensor_copy(key_scales[:], key_pool_scales[:].indirect(offsets[:]))
-        (query_mx,) = quantise("query", [query_raw])
+        query_scales = sb.tile([P, ROWS], U8, name="query_scales", align_bytes=64)
+        (query_mx,) = quantise("query_codes", round_and_group("query_bf16", [query_raw]), query_scales)
         halves = [slice(0, HALF), slice(HALF, SLOTS)]
         score = [ps.tile([P, HALF], F32, name="score%d" % h) for h in range(2)]
         for h, cols in enumerate(halves):
@@ -113,8 +118,8 @@ def tile_attend_hvdirect_dampened_s_kernel(
             product(score[h][:], query_mx, key_words[:, cols], key_scales[:, cols])
         base_sb = sb.tile([P, TOKENS], F32, name="base_sb", tag="key_pool_bytes", align_bytes=64)
         nc.sync.dma_start(out=base_sb[:], in_=base)
-        neg_a = wide("neg_a")
-        neg_max_first = sb.tile([P, 1], F32, name="neg_max_first", tag="first_max_bytes", align_bytes=64)
+        neg_a = sb.tile([P, SLOTS], F32, name="neg_a", tag="neg_a_bytes")
+        neg_max_first = column("neg_max_first")
         neg_max = column("neg_max")
         nc.vector.tensor_scalar(
             out=neg_a[:, halves[0]], in0=score[0][:], scalar1=-1.0, scalar2=None,
@@ -124,17 +129,19 @@ def tile_attend_hvdirect_dampened_s_kernel(
             out=neg_a[:, halves[1]], in0=score[1][:], scalar1=-1.0, scalar2=neg_max_first[:],
             op0=ALU.mult, op1=ALU.min, accum_out=neg_max[:],
         )
-        val_scales = sb.tile([P, SLOTS], U8, name="val_scales", tag="first_max_bytes", align_bytes=64)
+        val_scales = sb.tile([P, SLOTS], U8, name="val_scales", align_bytes=64)
         nc.vector.tensor_copy(val_scales[:], val_pool_scales[:].indirect(offsets[:]))
-        dquery_mx, gout_mx = quantise("dquery_gout", [dquery_raw, gout_raw])
-        ta = ps.tile([P, SLOTS], F32, name="ta")
-        product(ta[:], dquery_mx, key_words[:], key_scales[:])
+        dquery_gout_bf16 = round_and_group("dquery_gout_bf16", [dquery_raw, gout_raw])
 
         p = sb.tile([P, SLOTS], F32, name="p", tag="gout_raw")
         p_sum = column("p_sum")
         nc.scalar.activation(out=p[:], in_=neg_a[:], func=ACT.Exp, scale=-1.0, bias=neg_max[:], accum_out=p_sum[:])
-        inv_p = sb.tile([P, 1], F32, name="inv_p", tag="val_scale_bytes", align_bytes=64)
+        inv_p = reused.tile([P, 1], F32, name="inv_p", align_bytes=64, offset=0)
         nc.vector.reciprocal(out=inv_p[:], in_=p_sum[:])
+        dquery_gout_scales = reused.tile([P, 2 * ROWS], U8, name="dquery_gout_scales", align_bytes=64, offset=64)
+        dquery_mx, gout_mx = quantise("dquery_gout_codes", dquery_gout_bf16, dquery_gout_scales)
+        ta = ps.tile([P, SLOTS], F32, name="ta")
+        product(ta[:], dquery_mx, key_words[:], key_scales[:])
         k = column("k")
         neg_inv_p = column("neg_inv_p")
         nc.vector.tensor_scalar(out=k[:], in0=inv_p[:], scalar1=damp_sb[:], scalar2=512.0, op0=ALU.mult, op1=ALU.mult)
@@ -148,37 +155,39 @@ def tile_attend_hvdirect_dampened_s_kernel(
         c0 = ps.tile([P, SLOTS], F32, name="c0")
         product(c0[:], gout_mx, val_words[:], val_scales[:])
 
-        after_gather = sb.tile([P, 2 * SLOTS + 8], F32, name="after_gather", tag="val_pool_bytes", align_bytes=64)
+        after_gather = sb.tile([P, SLOTS + 8], F32, name="after_gather", tag="val_pool_bytes", align_bytes=64)
         neg_s_ta = after_gather[:, 0:SLOTS]
-        u0_less_a = after_gather[:, SLOTS : 2 * SLOTS]
-        inv_u = after_gather[:, 2 * SLOTS : 2 * SLOTS + 1]
+        u0_less_a = wide("u0_less_a")
+        inv_u = after_gather[:, SLOTS : SLOTS + 1]
         neg_t = column("neg_t")
         nc.vector.scalar_tensor_tensor(
             out=neg_s_ta, in0=ta[:], scalar=neg_inv_p[:], in1=p[:], op0=ALU.mult, op1=ALU.mult, accum_out=neg_t[:]
         )
         nc.vector.reciprocal(out=inv_u, in_=u_sum[:])
-        nc.vector.tensor_tensor(out=u0_less_a, in0=neg_a[:], in1=u0[:], op=ALU.add)
+        nc.gpsimd.tensor_tensor(out=u0_less_a[:], in0=neg_a[:], in1=u0[:], op=ALU.add)
         pw = wide("pw")
         pw_sum = column("pw_sum")
-        w = wide("w")
+        w = sb.tile([P, SLOTS], F32, name="w", tag="neg_a_bytes")
         nc.scalar.activation(
-            out=pw[:], in_=u0_less_a, func=ACT.Exp, scale=-1.0, bias=neg_max[:], accum_out=pw_sum[:]
+            out=pw[:], in_=u0_less_a[:], func=ACT.Exp, scale=-1.0, bias=neg_max[:], accum_out=pw_sum[:]
         )
         nc.scalar.activation(out=w[:], in_=u0[:], func=ACT.Exp, scale=-1.0)
 
         c = column("c")
-        neg_kappa = column("neg_kappa")
+        neg_ck = column("neg_ck")
+        ck_over_p = column("ck_over_p")
+        t_over_p = column("t_over_p")
         m = column("m")
         c0_u0 = wide("c0_u0")
+        c_tau = wide("c_tau")
+        nc.vector.tensor_scalar(out=t_over_p[:], in0=neg_t[:], scalar1=neg_inv_p[:], scalar2=None, op0=ALU.mult)
+        nc.vector.tensor_scalar(out=c[:], in0=inv_u, scalar1=k[:], scalar2=512.0, op0=ALU.mult, op1=ALU.mult)
         nc.vector.scalar_tensor_tensor(
             out=c0_u0[:], in0=c0[:], scalar=inv_u, in1=u0[:], op0=ALU.mult, op1=ALU.mult, accum_out=m[:]
         )
-        nc.vector.tensor_scalar(out=c[:], in0=inv_u, scalar1=k[:], scalar2=512.0, op0=ALU.mult, op1=ALU.mult)
-        nc.vector.tensor_scalar(out=neg_kappa[:], in0=inv_u, scalar1=k[:], scalar2=-1.0, op0=ALU.mult, op1=ALU.mult)
-        kappa_over_p = column("kappa_over_p")
-        t_over_p = column("t_over_p")
-        nc.vector.tensor_scalar(out=t_over_p[:], in0=neg_t[:], scalar1=neg_inv_p[:], scalar2=None, op0=ALU.mult)
-        nc.vector.tensor_scalar(out=kappa_over_p[:], in0=neg_kappa[:], scalar1=neg_inv_p[:], scalar2=None, op0=ALU.mult)
+        nc.vector.tensor_scalar(out=neg_ck[:], in0=c[:], scalar1=c[:], scalar2=-1.0 / 512.0, op0=ALU.mult, op1=ALU.mult)
+        nc.vector.tensor_scalar(out=c_tau[:], in0=ta[:], scalar1=neg_t[:], scalar2=c[:], op0=ALU.add, op1=ALU.mult)
+        nc.vector.tensor_scalar(out=ck_over_p[:], in0=neg_ck[:], scalar1=neg_inv_p[:], scalar2=None, op0=ALU.mult)
 
         def affine(name, x, scale, bias=None):
             y = column(name)
@@ -188,26 +197,28 @@ def tile_attend_hvdirect_dampened_s_kernel(
                 nc.scalar.activation(out=y[:], in_=x[:], func=ACT.Identity, scale=scale[:], bias=bias[:])
             return y
 
-        y2, y1, y1c, y3, z, j_term = wide("y2"), wide("y1"), wide("y1c"), wide("y3"), wide("z"), wide("j_term")
-        tu_sum, coef_ta, tm_sum, j_sum = column("tu_sum"), column("coef_ta"), column("tm_sum"), column("j_sum")
-        nc.vector.scalar_tensor_tensor(out=y1[:], in0=c0[:], scalar=m[:], in1=pw[:], op0=ALU.subtract, op1=ALU.mult)
-        nc.scalar.activation(out=y1c[:], in_=y1[:], func=ACT.Copy, scale=c[:], accum_out=coef_ta[:])
+        y2, y1, y3, z, j_term = wide("y2"), wide("y1"), wide("y3"), wide("z"), wide("j_term")
+        tu_sum, h_sum, tm_sum, j_sum = column("tu_sum"), column("h_sum"), column("tm_sum"), column("j_sum")
+        nc.gpsimd.tensor_tensor(out=z[:], in0=c_tau[:], in1=w[:], op=ALU.mult)
+        nc.vector.scalar_tensor_tensor(
+            out=y1[:], in0=c0[:], scalar=m[:], in1=pw[:], op0=ALU.subtract, op1=ALU.mult, accum_out=h_sum[:]
+        )
         nc.vector.scalar_tensor_tensor(
             out=y2[:], in0=ta[:], scalar=neg_t[:], in1=pw[:], op0=ALU.add, op1=ALU.mult, accum_out=tu_sum[:]
         )
-        nc.vector.scalar_tensor_tensor(out=z[:], in0=ta[:], scalar=neg_t[:], in1=w[:], op0=ALU.add, op1=ALU.mult)
         nc.vector.scalar_tensor_tensor(
-            out=y3[:], in0=ta[:], scalar=neg_t[:], in1=y1c[:], op0=ALU.add, op1=ALU.mult, accum_out=tm_sum[:]
+            out=y3[:], in0=ta[:], scalar=neg_t[:], in1=y1[:], op0=ALU.add, op1=ALU.mult, accum_out=tm_sum[:]
         )
-        coef_y1 = affine("coef_y1", tu_sum, neg_kappa)
-        per_tm = affine("per_tm", pw_sum, kappa_over_p)
-        part1 = affine("part1", coef_ta, t_over_p)
+        per_tm = affine("per_tm", pw_sum, ck_over_p)
+        coef_ta = affine("coef_ta", h_sum, c)
+        coef_y1 = affine("coef_y1", tu_sum, neg_ck)
         ta_term = wide("ta_term")
         nc.scalar.activation(out=ta_term[:], in_=neg_s_ta, func=ACT.Copy, scale=coef_ta[:])
+        part1 = affine("part1", coef_ta, t_over_p)
         nc.vector.scalar_tensor_tensor(
-            out=j_term[:], in0=z[:], scalar=coef_y1[:], in1=y1c[:], op0=ALU.add, op1=ALU.mult, accum_out=j_sum[:]
+            out=j_term[:], in0=z[:], scalar=coef_y1[:], in1=y1[:], op0=ALU.add, op1=ALU.mult, accum_out=j_sum[:]
         )
-        coef_pw = affine("coef_pw", tm_sum, neg_kappa)
+        coef_pw = affine("coef_pw", tm_sum, neg_ck)
         part2 = affine("part2", tm_sum, per_tm, part1)
         coef_p = affine("coef_p", j_sum, neg_inv_p, part2)
 

from contextlib import ExitStack

import concourse.mybir as mybir

F32 = mybir.dt.float32
BF16 = mybir.dt.bfloat16
I32 = mybir.dt.int32
U32 = mybir.dt.uint32
U16 = mybir.dt.uint16
U8 = mybir.dt.uint8
FP8X4 = mybir.dt.float8_e4m3fn_x4
ALU = mybir.AluOpType
ACT = mybir.ActivationFunctionType

P = 128
PACK = 4
TOKENS = 2048
SLOTS = 512
ROWS = 128
HALF = SLOTS // 2
OUT_EDGES = (0, 256, 768, 1280, 1792, 2048)

FLOPS = 3 * 2 * 512 * ROWS * SLOTS


def tile_attend_hvdirect_dampened_s_kernel(
    tc, query, keys_words, keys_scales, damp, gout, vals_words, vals_scales, dquery, base, offs, out
):
    nc = tc.nc
    with ExitStack() as ctx:
        sb = ctx.enter_context(tc.tile_pool(name="sb", bufs=1))
        reused = ctx.enter_context(tc.tile_pool(name="reused", bufs=1))
        ps = ctx.enter_context(tc.psum_pool(name="ps", bufs=1))

        def wide(name):
            return sb.tile([P, SLOTS], F32, name=name)

        def column(name):
            return sb.tile([P, 1], F32, name=name)

        def load_scale_rows(plane, rows):
            for quad in range(4):
                nc.sync.dma_start(
                    out=plane[32 * quad : 32 * quad + 4, :].bitcast(I32),
                    in_=rows[0, 4 * quad : 4 * quad + 4, :].bitcast(I32),
                )

        def load_words(pool_words, words):
            nc.sync.dma_start(
                out=pool_words[:].bitcast(I32), in_=words[0].rearrange("p n t -> p (n t)").bitcast(I32)
            )

        def load_rows(name, matrix):
            raw = sb.tile([P, PACK, ROWS], F32, name=name, tag=name)
            nc.sync.dma_start(out=raw[:], in_=matrix.rearrange("(p j) w -> p j w", j=PACK))
            return raw

        def round_and_group(name, raws):
            grouped = sb.tile([P, ROWS * len(raws), PACK], BF16, name=name, align_bytes=64)
            for i, raw in enumerate(raws):
                nc.scalar.activation(
                    out=grouped[:, ROWS * i : ROWS * (i + 1), :], in_=raw[:].rearrange("p j w -> p w j"), func=ACT.Copy
                )
            return grouped

        def quantise(name, grouped, scales):
            width = grouped.shape[1]
            codes = sb.tile([P, width], U32, name=name, align_bytes=64)
            nc.vector.quantize_mx(
                out=codes[:].bitcast(FP8X4), scales=scales[:], in_=grouped[:].rearrange("p w j -> p (w j)")
            )
            return [(codes[:, s : s + ROWS], scales[:, s : s + ROWS]) for s in range(0, width, ROWS)]

        def product(acc, stationary, words, scales):
            nc.tensor.matmul_mx(
                out=acc,
                lhsT=stationary[0].bitcast(FP8X4),
                lhsT_scale=stationary[1],
                rhs=words.bitcast(FP8X4),
                rhs_scale=scales,
                start=True,
                stop=True,
            )

        offsets = sb.tile([P, SLOTS // 16], U16, name="offsets")
        key_pool = sb.tile([P, TOKENS], U32, name="key_pool", tag="key_pool_bytes", align_bytes=64)
        key_pool_scales = sb.tile([P, TOKENS], U8, name="key_pool_scales", align_bytes=64)
        val_pool = sb.tile([P, TOKENS], U32, name="val_pool", tag="val_pool_bytes", align_bytes=64)
        val_pool_scales = reused.tile([P, TOKENS], U8, name="val_pool_scales", align_bytes=64, offset=0)
        placed = sb.tile([P, TOKENS], F32, name="placed")
        damp_sb = column("damp_sb")

        nc.vector.memset(key_pool_scales[:].bitcast(I32), 0)
        nc.vector.memset(val_pool_scales[:].bitcast(I32), 0)
        nc.vector.memset(placed[:], 0.0)

        nc.gpsimd.dma_start(out=damp_sb[:], in_=damp)
        nc.sync.dma_start(offsets[:], offs)
        query_raw = load_rows("query_raw", query)
        load_scale_rows(key_pool_scales, keys_scales)
        load_words(key_pool, keys_words)
        dquery_raw = load_rows("dquery_raw", dquery)
        gout_raw = load_rows("gout_raw", gout)
        load_scale_rows(val_pool_scales, vals_scales)
        load_words(val_pool, vals_words)

        key_words = sb.tile([P, SLOTS], U32, name="key_words", align_bytes=64)
        key_scales = sb.tile([P, SLOTS], U8, name="key_scales", align_bytes=64)
        nc.vector.tensor_copy(key_scales[:], key_pool_scales[:].indirect(offsets[:]))
        query_scales = sb.tile([P, ROWS], U8, name="query_scales", align_bytes=64)
        (query_mx,) = quantise("query_codes", round_and_group("query_bf16", [query_raw]), query_scales)
        halves = [slice(0, HALF), slice(HALF, SLOTS)]
        score = [ps.tile([P, HALF], F32, name="score%d" % h) for h in range(2)]
        for h, cols in enumerate(halves):
            nc.vector.tensor_copy(
                key_words[:, cols], key_pool[:].indirect(offsets[:, cols.start // 16 : cols.stop // 16])
            )
            product(score[h][:], query_mx, key_words[:, cols], key_scales[:, cols])
        base_sb = sb.tile([P, TOKENS], F32, name="base_sb", tag="key_pool_bytes", align_bytes=64)
        nc.sync.dma_start(out=base_sb[:], in_=base)
        neg_a = sb.tile([P, SLOTS], F32, name="neg_a", tag="neg_a_bytes")
        neg_max_first = column("neg_max_first")
        neg_max = column("neg_max")
        nc.vector.tensor_scalar(
            out=neg_a[:, halves[0]], in0=score[0][:], scalar1=-1.0, scalar2=None,
            op0=ALU.mult, op1=ALU.min, accum_out=neg_max_first[:],
        )
        nc.vector.tensor_scalar(
            out=neg_a[:, halves[1]], in0=score[1][:], scalar1=-1.0, scalar2=neg_max_first[:],
            op0=ALU.mult, op1=ALU.min, accum_out=neg_max[:],
        )
        val_scales = sb.tile([P, SLOTS], U8, name="val_scales", align_bytes=64)
        nc.vector.tensor_copy(val_scales[:], val_pool_scales[:].indirect(offsets[:]))
        dquery_gout_bf16 = round_and_group("dquery_gout_bf16", [dquery_raw, gout_raw])

        p = sb.tile([P, SLOTS], F32, name="p", tag="gout_raw")
        p_sum = column("p_sum")
        nc.scalar.activation(out=p[:], in_=neg_a[:], func=ACT.Exp, scale=-1.0, bias=neg_max[:], accum_out=p_sum[:])
        inv_p = reused.tile([P, 1], F32, name="inv_p", align_bytes=64, offset=0)
        nc.vector.reciprocal(out=inv_p[:], in_=p_sum[:])
        dquery_gout_scales = reused.tile([P, 2 * ROWS], U8, name="dquery_gout_scales", align_bytes=64, offset=64)
        dquery_mx, gout_mx = quantise("dquery_gout_codes", dquery_gout_bf16, dquery_gout_scales)
        ta = ps.tile([P, SLOTS], F32, name="ta")
        product(ta[:], dquery_mx, key_words[:], key_scales[:])
        k = column("k")
        neg_inv_p = column("neg_inv_p")
        nc.vector.tensor_scalar(out=k[:], in0=inv_p[:], scalar1=damp_sb[:], scalar2=512.0, op0=ALU.mult, op1=ALU.mult)
        u0 = wide("u0")
        u_sum = column("u_sum")
        nc.scalar.activation(out=u0[:], in_=p[:], func=ACT.Ln, scale=k[:], bias=1.0, accum_out=u_sum[:])

        nc.vector.tensor_scalar(out=neg_inv_p[:], in0=inv_p[:], scalar1=-1.0, scalar2=None, op0=ALU.mult)
        val_words = sb.tile([P, SLOTS], U32, name="val_words", align_bytes=64)
        nc.vector.tensor_copy(val_words[:], val_pool[:].indirect(offsets[:]))
        c0 = ps.tile([P, SLOTS], F32, name="c0")
        product(c0[:], gout_mx, val_words[:], val_scales[:])

        after_gather = sb.tile([P, SLOTS + 8], F32, name="after_gather", tag="val_pool_bytes", align_bytes=64)
        neg_s_ta = after_gather[:, 0:SLOTS]
        u0_less_a = wide("u0_less_a")
        inv_u = after_gather[:, SLOTS : SLOTS + 1]
        neg_t = column("neg_t")
        nc.vector.scalar_tensor_tensor(
            out=neg_s_ta, in0=ta[:], scalar=neg_inv_p[:], in1=p[:], op0=ALU.mult, op1=ALU.mult, accum_out=neg_t[:]
        )
        nc.vector.reciprocal(out=inv_u, in_=u_sum[:])
        nc.gpsimd.tensor_tensor(out=u0_less_a[:], in0=neg_a[:], in1=u0[:], op=ALU.add)
        pw = wide("pw")
        pw_sum = column("pw_sum")
        w = sb.tile([P, SLOTS], F32, name="w", tag="neg_a_bytes")
        nc.scalar.activation(
            out=pw[:], in_=u0_less_a[:], func=ACT.Exp, scale=-1.0, bias=neg_max[:], accum_out=pw_sum[:]
        )
        nc.scalar.activation(out=w[:], in_=u0[:], func=ACT.Exp, scale=-1.0)

        c = column("c")
        neg_ck = column("neg_ck")
        ck_over_p = column("ck_over_p")
        t_over_p = column("t_over_p")
        m = column("m")
        c0_u0 = wide("c0_u0")
        c_tau = wide("c_tau")
        nc.vector.tensor_scalar(out=t_over_p[:], in0=neg_t[:], scalar1=neg_inv_p[:], scalar2=None, op0=ALU.mult)
        nc.vector.tensor_scalar(out=c[:], in0=inv_u, scalar1=k[:], scalar2=512.0, op0=ALU.mult, op1=ALU.mult)
        nc.vector.scalar_tensor_tensor(
            out=c0_u0[:], in0=c0[:], scalar=inv_u, in1=u0[:], op0=ALU.mult, op1=ALU.mult, accum_out=m[:]
        )
        nc.vector.tensor_scalar(out=neg_ck[:], in0=c[:], scalar1=c[:], scalar2=-1.0 / 512.0, op0=ALU.mult, op1=ALU.mult)
        nc.vector.tensor_scalar(out=c_tau[:], in0=ta[:], scalar1=neg_t[:], scalar2=c[:], op0=ALU.add, op1=ALU.mult)
        nc.vector.tensor_scalar(out=ck_over_p[:], in0=neg_ck[:], scalar1=neg_inv_p[:], scalar2=None, op0=ALU.mult)

        def affine(name, x, scale, bias=None):
            y = column(name)
            if bias is None:
                nc.scalar.activation(out=y[:], in_=x[:], func=ACT.Copy, scale=scale[:])
            else:
                nc.scalar.activation(out=y[:], in_=x[:], func=ACT.Identity, scale=scale[:], bias=bias[:])
            return y

        y2, y1, y3, z, j_term = wide("y2"), wide("y1"), wide("y3"), wide("z"), wide("j_term")
        tu_sum, h_sum, tm_sum, j_sum = column("tu_sum"), column("h_sum"), column("tm_sum"), column("j_sum")
        nc.gpsimd.tensor_tensor(out=z[:], in0=c_tau[:], in1=w[:], op=ALU.mult)
        nc.vector.scalar_tensor_tensor(
            out=y1[:], in0=c0[:], scalar=m[:], in1=pw[:], op0=ALU.subtract, op1=ALU.mult, accum_out=h_sum[:]
        )
        nc.vector.scalar_tensor_tensor(
            out=y2[:], in0=ta[:], scalar=neg_t[:], in1=pw[:], op0=ALU.add, op1=ALU.mult, accum_out=tu_sum[:]
        )
        nc.vector.scalar_tensor_tensor(
            out=y3[:], in0=ta[:], scalar=neg_t[:], in1=y1[:], op0=ALU.add, op1=ALU.mult, accum_out=tm_sum[:]
        )
        per_tm = affine("per_tm", pw_sum, ck_over_p)
        coef_ta = affine("coef_ta", h_sum, c)
        coef_y1 = affine("coef_y1", tu_sum, neg_ck)
        ta_term = wide("ta_term")
        nc.scalar.activation(out=ta_term[:], in_=neg_s_ta, func=ACT.Copy, scale=coef_ta[:])
        part1 = affine("part1", coef_ta, t_over_p)
        nc.vector.scalar_tensor_tensor(
            out=j_term[:], in0=z[:], scalar=coef_y1[:], in1=y1[:], op0=ALU.add, op1=ALU.mult, accum_out=j_sum[:]
        )
        coef_pw = affine("coef_pw", tm_sum, neg_ck)
        part2 = affine("part2", tm_sum, per_tm, part1)
        coef_p = affine("coef_p", j_sum, neg_inv_p, part2)

        f1, f2 = wide("f1"), wide("f2")
        nc.vector.scalar_tensor_tensor(out=f1[:], in0=pw[:], scalar=coef_pw[:], in1=ta_term[:], op0=ALU.mult, op1=ALU.add)
        nc.vector.scalar_tensor_tensor(out=f2[:], in0=p[:], scalar=coef_p[:], in1=j_term[:], op0=ALU.mult, op1=ALU.add)
        nc.vector.tensor_tensor(out=placed[:].indirect(offsets[:]), in0=f1[:], in1=f2[:], op=ALU.add)

        for j in range(len(OUT_EDGES) - 1):
            cols = slice(OUT_EDGES[j], OUT_EDGES[j + 1])
            result = sb.tile([P, cols.stop - cols.start], F32, name="result%d" % j)
            nc.vector.tensor_tensor(out=result[:], in0=base_sb[:, cols], in1=placed[:, cols], op=ALU.add)
            nc.sync.dma_start(out=out[:, cols], in_=result[:])
